import numpy as np, ml_dtypes
CORES = [9,10,11,14,17,18,19,22,49,50,51,54]
N = 12
KB, QP = 4, 128
MEM = [3]
def setup_inputs(rng):
    return {"q": rng.standard_normal((N, 128, QP), dtype=np.float32).astype(ml_dtypes.bfloat16), "k": rng.standard_normal((N, 128, KB * 128), dtype=np.float32).astype(ml_dtypes.bfloat16), "v": rng.standard_normal((N, 128, KB * 128), dtype=np.float32).astype(ml_dtypes.bfloat16)}
def setup_inputs_big(rng):
    d = setup_inputs(rng)
    for k in ("q", "k", "v"): d[k] = (d[k].astype(np.float32) * 1024.0).astype(d[k].dtype)
    return d
def setup_inputs_small(rng):
    d = setup_inputs(rng)
    for k in ("q", "k", "v"): d[k] = (d[k].astype(np.float32) * (1 / 1024.0)).astype(d[k].dtype)
    return d
def setup_inputs_apart(rng):
    d = setup_inputs(rng)
    f = (10.0 ** rng.permutation(np.linspace(-1.5, 1.5, N))).astype(np.float32).reshape(N, 1, 1)
    for k in ("q", "k", "v"): d[k] = (d[k].astype(np.float32) * f).astype(d[k].dtype)
    return d
def reference(q, k, v):
    Q, K, V = q.astype(np.float64), k.astype(np.float64), v.astype(np.float64)
    y = np.zeros((N, 128, QP))
    for r in range(N):
        for j in MEM:
            for b in range(KB):
                S = np.maximum(K[j][:, 128 * b:128 * b + 128].T @ Q[r], 0.0)
                y[r] += V[j][:, 128 * b:128 * b + 128].T @ S
    return {"y": y.astype(ml_dtypes.bfloat16 if q.dtype != np.float64 else np.float64)}

@@ -1,0 +1,184 @@
+from concourse.mybir import AluOpType
+
+NR = 12
+NSIM = 64
+D = 128
+KB = 4
+NHELP = 1
+NMEM_FAR = 3
+NE_Q = 8
+NE_RELAY = 4
+NE_KV = 16
+NE_Y = 8
+NBANK = 4
+
+SCRATCH = {
+    "kv": ("sbuf", [D, 2 * KB * D], "bfloat16"),
+    "qin": ("sbuf", [D, NR * D], "bfloat16"),
+    "sact": ("sbuf", [D, NR * KB * D], "bfloat16"),
+    "yo": ("sbuf", [D, NR * D], "bfloat16"),
+    "zero": ("sbuf", [D, KB * D], "float32"),
+    "qd": ("dram", [D, D], "bfloat16"),
+    "qr": ("dram", [D, D], "bfloat16"),
+    "yd": ("dram", [D, D], "bfloat16"),
+}
+for _b in range(NBANK):
+    SCRATCH["ps%d" % _b] = ("psum", [D, 512], "float32")
+    SCRATCH["po%d" % _b] = ("psum", [D, 512], "float32")
+
+SEMAPHORES = ["kvld", "kvar", "qld", "qrel", "zr", "sent", "yarr", "st"]
+SEMAPHORES += ["qa%d" % r for r in range(NR)]
+SEMAPHORES += ["%s%d" % (s, i) for s in ("sS", "sR", "sO", "sY") for i in range(NR)]
+
+
+def _pick(mask, n, avoid=0):
+    bits = [b for b in range(mask.bit_length()) if (mask >> b) & 1]
+    bits.sort(key=lambda b: ((avoid >> b) & 1, b))
+    m = 0
+    for b in bits[:n]:
+        m |= 1 << b
+    return m
+
+
+def _plan(T, topo):
+    cores = list(T.cores)
+    mem = cores[T.tables["MEM"][0]]
+    home = topo.chip(mem)
+    near = [c for c in cores if c != mem and topo.chip(c) == home]
+    far = [c for c in cores if topo.chip(c) != home]
+    cand = [c for c in range(NSIM) if topo.chip(c) == home and c not in cores
+            and all(topo.may_write(c, f) for f in far)]
+    cand.sort(key=lambda c: (topo.die(c) != topo.die(mem), c))
+    helpers = cand[:NHELP]
+    direct = [c for c in far if topo.may_write(c, mem)]
+    indirect = [c for c in far if not topo.may_write(c, mem)]
+    relay = {}
+    for c in indirect:
+        opts = [d for d in direct if topo.chip(d) == topo.chip(c)]
+        relay[c] = min(opts, key=lambda d: (sum(1 for x in opts if topo.die(x) == topo.die(d)), d))
+    pos = {}
+    for c in direct:
+        pos[c] = sum(1 for x in direct if topo.chip(x) == topo.chip(c) and x < c)
+    direct = sorted(direct, key=lambda c: (c in relay.values(), pos[c], c))
+    serve = {mem: [[mem], near + direct[:NMEM_FAR]]}
+    rest = direct[NMEM_FAR:]
+    for j, h in enumerate(helpers):
+        serve[h] = [rest[j::len(helpers)], indirect[j::len(helpers)]]
+    server = {}
+    for s in serve:
+        for w in serve[s]:
+            for c in w:
+                server[c] = s
+    return {"mem": mem, "helpers": helpers, "far": far, "relay": relay, "serve": serve, "server": server}
+
+
+def rank_program(g, core, T, topo):
+    P = _plan(T, topo)
+    rank = T.rank_of(core)
+    if rank is None and core not in P["serve"]:
+        return
+    sem = T.sem
+    mem = P["mem"]
+    sent = [0]
+    stored = [0]
+
+    def write(dst, out_ap, in_ap, remote_sem, n, avoid=0):
+        rid, pid, _se = topo.addr(dst)
+        g.remote_dma(out_ap=out_ap, in_ap=in_ap, remote_sem=remote_sem, local_sem=sem.sent, pid=pid, routing_id=rid,
+                     dma_engine_mask=_pick(topo.mask(core, dst), n, avoid))
+        sent[0] += n
+
+    def qslot(r):
+        return T.qin[:, r * D:(r + 1) * D]
+
+    if core in P["serve"]:
+        waves = [w for w in P["serve"][core] if w]
+        order = [c for w in waves for c in w]
+        if core == mem:
+            g.sync.dma_start(T.kv[:, 0:KB * D], T.k[:]).then_inc(sem.kvld, 16)
+            g.scalar.dma_start(T.kv[:, KB * D:2 * KB * D], T.v[:]).then_inc(sem.kvld, 16)
+            kv_sem, kv_cnt = sem.kvld, 32
+        else:
+            kv_sem, kv_cnt = sem.kvar, NE_KV
+        if core in order:
+            g.sync.dma_start(qslot(rank), T.q[:]).then_inc(sem.qld, 16)
+        g.vector.memset(T.zero[:], 0.0).then_inc(sem.zr, 1)
+        g.vector.wait_ge(sem.zr, 1)
+        g.tensor.wait_ge(kv_sem, kv_cnt)
+
+        def scores(i):
+            c = order[i]
+            r = T.rank_of(c)
+            if c == core:
+                g.tensor.wait_ge(sem.qld, 16)
+            else:
+                g.tensor.wait_ge(sem["qa%d" % r], NE_Q)
+            ps = T["ps%d" % (i % NBANK)]
+            for b in range(KB):
+                g.tensor.matmul(ps[:, b * D:(b + 1) * D], T.kv[:, b * D:(b + 1) * D], qslot(r),
+                                start=True, stop=True).then_inc(sem["sS%d" % i], 1)
+
+        def clamp(i):
+            g.vector.wait_ge(sem["sS%d" % i], KB)
+            g.vector.tensor_tensor(T.sact[:, i * KB * D:(i + 1) * KB * D], T["ps%d" % (i % NBANK)][:], T.zero[:],
+                                   AluOpType.max).then_inc(sem["sR%d" % i], 1)
+
+        def outs(i):
+            g.tensor.wait_ge(sem["sR%d" % i], 1)
+            if i >= NBANK:
+                g.tensor.wait_ge(sem["sY%d" % (i - NBANK)], 1)
+            po = T["po%d" % (i % NBANK)]
+            for b in range(KB):
+                g.tensor.matmul(po[:, 0:D], T.kv[:, (KB + b) * D:(KB + b + 1) * D],
+                                T.sact[:, (i * KB + b) * D:(i * KB + b + 1) * D],
+                                start=(b == 0), stop=(b == KB - 1)).then_inc(sem["sO%d" % i], 1)
+
+        def result(i):
+            g.vector.wait_ge(sem["sO%d" % i], KB)
+            g.vector.tensor_copy(T.yo[:, i * D:(i + 1) * D], T["po%d" % (i % NBANK)][:, 0:D]).then_inc(
+                sem["sY%d" % i], 1)
+
+        base = 0
+        for w in waves:
+            for j in range(len(w) + 1):
+                if j < len(w):
+                    scores(base + j)
+                    clamp(base + j)
+                if j >= 1:
+                    outs(base + j - 1)
+                    result(base + j - 1)
+            base += len(w)
+        if core == mem and P["helpers"]:
+            g.wait_ge(sem.kvld, 32)
+            for h in P["helpers"]:
+                write(h, T.kv[:], T.kv[:], sem.kvar, NE_KV)
+        far_mask = topo.mask(core, P["far"][0])
+        for i, c in enumerate(order):
+            if c == core:
+                g.sync.wait_ge(sem["sY%d" % i], 1)
+                g.sync.dma_start(T.y[:], T.yo[:, i * D:(i + 1) * D]).then_inc(sem.st, 16)
+                stored[0] += 16
+            else:
+                g.wait_ge(sem["sY%d" % i], 1)
+                write(c, T.yd[:], T.yo[:, i * D:(i + 1) * D], sem.yarr, NE_Y,
+                      avoid=far_mask if topo.chip(c) == topo.chip(core) else 0)
+
+    if rank is not None and P["server"][core] != core:
+        g.sync.dma_start(T.qd[:], T.q[:]).then_inc(sem.qld, 16)
+        g.wait_ge(sem.qld, 16)
+        if core in P["relay"]:
+            write(P["relay"][core], T.qr[:], T.qd[:], sem.qrel, NE_RELAY)
+        else:
+            write(P["server"][core], qslot(rank), T.qd[:], sem["qa%d" % rank], NE_Q)
+        for c in P["relay"]:
+            if P["relay"][c] == core:
+                g.wait_ge(sem.qrel, NE_RELAY)
+                write(P["server"][c], qslot(T.rank_of(c)), T.qr[:], sem["qa%d" % T.rank_of(c)], NE_Q)
+        g.sync.wait_ge(sem.yarr, NE_Y)
+        g.sync.dma_start(T.y[:], T.yd[:]).then_inc(sem.st, 16)
+        stored[0] += 16
+
+    if sent[0]:
+        g.wait_ge(sem.sent, sent[0])
+    if stored[0]:
+        g.wait_ge(sem.st, stored[0])

@@ -4,8 +4,8 @@ NR = 12
 NSIM = 64
 D = 128
 KB = 4
-NHELP = 1
-NMEM_FAR = 3
+NHELP = 2
+NMEM_FAR = 1
 NE_Q = 8
 NE_RELAY = 4
 NE_KV = 16
@@ -13,7 +13,8 @@ NE_Y = 8
 NBANK = 4
 
 SCRATCH = {
-    "kv": ("sbuf", [D, 2 * KB * D], "bfloat16"),
+    "kk": ("sbuf", [D, KB * D], "bfloat16"),
+    "vv": ("sbuf", [D, KB * D], "bfloat16"),
     "qin": ("sbuf", [D, NR * D], "bfloat16"),
     "sact": ("sbuf", [D, NR * KB * D], "bfloat16"),
     "yo": ("sbuf", [D, NR * D], "bfloat16"),
@@ -26,7 +27,7 @@ for _b in range(NBANK):
     SCRATCH["ps%d" % _b] = ("psum", [D, 512], "float32")
     SCRATCH["po%d" % _b] = ("psum", [D, 512], "float32")
 
-SEMAPHORES = ["kvld", "kvar", "qld", "qrel", "zr", "sent", "yarr", "st"]
+SEMAPHORES = ["kld", "vld", "kar", "var", "qld", "qrel", "zr", "sent", "yarr", "st"]
 SEMAPHORES += ["qa%d" % r for r in range(NR)]
 SEMAPHORES += ["%s%d" % (s, i) for s in ("sS", "sR", "sO", "sY") for i in range(NR)]
 
@@ -46,9 +47,9 @@ def _plan(T, topo):
     home = topo.chip(mem)
     near = [c for c in cores if c != mem and topo.chip(c) == home]
     far = [c for c in cores if topo.chip(c) != home]
-    cand = [c for c in range(NSIM) if topo.chip(c) == home and c not in cores
+    cand = [c for c in range(NSIM) if topo.chip(c) == home and c != mem
             and all(topo.may_write(c, f) for f in far)]
-    cand.sort(key=lambda c: (topo.die(c) != topo.die(mem), c))
+    cand.sort(key=lambda c: (topo.die(c) == topo.die(mem), c))
     helpers = cand[:NHELP]
     direct = [c for c in far if topo.may_write(c, mem)]
     indirect = [c for c in far if not topo.may_write(c, mem)]
@@ -60,10 +61,16 @@ def _plan(T, topo):
     for c in direct:
         pos[c] = sum(1 for x in direct if topo.chip(x) == topo.chip(c) and x < c)
     direct = sorted(direct, key=lambda c: (c in relay.values(), pos[c], c))
-    serve = {mem: [[mem], near + direct[:NMEM_FAR]]}
+    first = {mem: near + direct[:NMEM_FAR]}
     rest = direct[NMEM_FAR:]
     for j, h in enumerate(helpers):
-        serve[h] = [rest[j::len(helpers)], indirect[j::len(helpers)]]
+        first[h] = rest[j::len(helpers)]
+    late = {s: [] for s in first}
+    turn = [mem] + helpers[::-1]
+    for k, c in enumerate(indirect):
+        late[turn[k % len(turn)]].append(c)
+    late[mem].append(mem)
+    serve = {s: [first[s], late[s]] for s in first}
     server = {}
     for s in serve:
         for w in serve[s]:
@@ -81,6 +88,7 @@ def rank_program(g, core, T, topo):
     mem = P["mem"]
     sent = [0]
     stored = [0]
+    client = rank is not None and P["server"][core] != core
 
     def write(dst, out_ap, in_ap, remote_sem, n, avoid=0):
         rid, pid, _se = topo.addr(dst)
@@ -91,20 +99,32 @@ def rank_program(g, core, T, topo):
     def qslot(r):
         return T.qin[:, r * D:(r + 1) * D]
 
+    if client:
+        g.sync.dma_start(T.qd[:], T.q[:]).then_inc(sem.qld, 16)
+        g.wait_ge(sem.qld, 16)
+        if core in P["relay"]:
+            write(P["relay"][core], T.qr[:], T.qd[:], sem.qrel, NE_RELAY)
+        else:
+            write(P["server"][core], qslot(rank), T.qd[:], sem["qa%d" % rank], NE_Q)
+        for c in P["relay"]:
+            if P["relay"][c] == core:
+                g.wait_ge(sem.qrel, NE_RELAY)
+                write(P["server"][c], qslot(T.rank_of(c)), T.qr[:], sem["qa%d" % T.rank_of(c)], NE_Q)
+
     if core in P["serve"]:
         waves = [w for w in P["serve"][core] if w]
         order = [c for w in waves for c in w]
         if core == mem:
-            g.sync.dma_start(T.kv[:, 0:KB * D], T.k[:]).then_inc(sem.kvld, 16)
-            g.scalar.dma_start(T.kv[:, KB * D:2 * KB * D], T.v[:]).then_inc(sem.kvld, 16)
-            kv_sem, kv_cnt = sem.kvld, 32
+            g.sync.dma_start(T.kk[:], T.k[:]).then_inc(sem.kld, 16)
+            g.sync.dma_start(T.vv[:], T.v[:]).then_inc(sem.vld, 16)
+            k_sem, v_sem, kv_cnt = sem.kld, sem.vld, 16
         else:
-            kv_sem, kv_cnt = sem.kvar, NE_KV
+            k_sem, v_sem, kv_cnt = sem.kar, sem.var, NE_KV
         if core in order:
             g.sync.dma_start(qslot(rank), T.q[:]).then_inc(sem.qld, 16)
         g.vector.memset(T.zero[:], 0.0).then_inc(sem.zr, 1)
         g.vector.wait_ge(sem.zr, 1)
-        g.tensor.wait_ge(kv_sem, kv_cnt)
+        g.tensor.wait_ge(k_sem, kv_cnt)
 
         def scores(i):
             c = order[i]
@@ -115,43 +135,41 @@ def rank_program(g, core, T, topo):
                 g.tensor.wait_ge(sem["qa%d" % r], NE_Q)
             ps = T["ps%d" % (i % NBANK)]
             for b in range(KB):
-                g.tensor.matmul(ps[:, b * D:(b + 1) * D], T.kv[:, b * D:(b + 1) * D], qslot(r),
+                g.tensor.matmul(ps[:, b * D:(b + 1) * D], T.kk[:, b * D:(b + 1) * D], qslot(r),
                                 start=True, stop=True).then_inc(sem["sS%d" % i], 1)
-
-        def clamp(i):
             g.vector.wait_ge(sem["sS%d" % i], KB)
-            g.vector.tensor_tensor(T.sact[:, i * KB * D:(i + 1) * KB * D], T["ps%d" % (i % NBANK)][:], T.zero[:],
+            g.vector.tensor_tensor(T.sact[:, i * KB * D:(i + 1) * KB * D], ps[:], T.zero[:],
                                    AluOpType.max).then_inc(sem["sR%d" % i], 1)
 
         def outs(i):
+            if i == 0:
+                g.tensor.wait_ge(v_sem, kv_cnt)
             g.tensor.wait_ge(sem["sR%d" % i], 1)
             if i >= NBANK:
                 g.tensor.wait_ge(sem["sY%d" % (i - NBANK)], 1)
             po = T["po%d" % (i % NBANK)]
             for b in range(KB):
-                g.tensor.matmul(po[:, 0:D], T.kv[:, (KB + b) * D:(KB + b + 1) * D],
+                g.tensor.matmul(po[:, 0:D], T.vv[:, b * D:(b + 1) * D],
                                 T.sact[:, (i * KB + b) * D:(i * KB + b + 1) * D],
                                 start=(b == 0), stop=(b == KB - 1)).then_inc(sem["sO%d" % i], 1)
-
-        def result(i):
             g.vector.wait_ge(sem["sO%d" % i], KB)
-            g.vector.tensor_copy(T.yo[:, i * D:(i + 1) * D], T["po%d" % (i % NBANK)][:, 0:D]).then_inc(
-                sem["sY%d" % i], 1)
+            g.vector.tensor_copy(T.yo[:, i * D:(i + 1) * D], po[:, 0:D]).then_inc(sem["sY%d" % i], 1)
 
         base = 0
         for w in waves:
             for j in range(len(w) + 1):
                 if j < len(w):
                     scores(base + j)
-                    clamp(base + j)
                 if j >= 1:
                     outs(base + j - 1)
-                    result(base + j - 1)
             base += len(w)
         if core == mem and P["helpers"]:
-            g.wait_ge(sem.kvld, 32)
+            g.wait_ge(sem.kld, 16)
             for h in P["helpers"]:
-                write(h, T.kv[:], T.kv[:], sem.kvar, NE_KV)
+                write(h, T.kk[:], T.kk[:], sem.kar, NE_KV)
+            g.wait_ge(sem.vld, 16)
+            for h in P["helpers"]:
+                write(h, T.vv[:], T.vv[:], sem.var, NE_KV)
         far_mask = topo.mask(core, P["far"][0])
         for i, c in enumerate(order):
             if c == core:
@@ -163,17 +181,7 @@ def rank_program(g, core, T, topo):
                 write(c, T.yd[:], T.yo[:, i * D:(i + 1) * D], sem.yarr, NE_Y,
                       avoid=far_mask if topo.chip(c) == topo.chip(core) else 0)
 
-    if rank is not None and P["server"][core] != core:
-        g.sync.dma_start(T.qd[:], T.q[:]).then_inc(sem.qld, 16)
-        g.wait_ge(sem.qld, 16)
-        if core in P["relay"]:
-            write(P["relay"][core], T.qr[:], T.qd[:], sem.qrel, NE_RELAY)
-        else:
-            write(P["server"][core], qslot(rank), T.qd[:], sem["qa%d" % rank], NE_Q)
-        for c in P["relay"]:
-            if P["relay"][c] == core:
-                g.wait_ge(sem.qrel, NE_RELAY)
-                write(P["server"][c], qslot(T.rank_of(c)), T.qr[:], sem["qa%d" % T.rank_of(c)], NE_Q)
+    if client:
         g.sync.wait_ge(sem.yarr, NE_Y)
         g.sync.dma_start(T.y[:], T.yd[:]).then_inc(sem.st, 16)
         stored[0] += 16

from concourse.mybir import AluOpType

NR = 12
NSIM = 64
D = 128
KB = 4
NHELP = 2
NMEM_FAR = 1
NE_Q = 8
NE_RELAY = 4
NE_KV = 16
NE_Y = 8
NBANK = 4

SCRATCH = {
    "kk": ("sbuf", [D, KB * D], "bfloat16"),
    "vv": ("sbuf", [D, KB * D], "bfloat16"),
    "qin": ("sbuf", [D, NR * D], "bfloat16"),
    "sact": ("sbuf", [D, NR * KB * D], "bfloat16"),
    "yo": ("sbuf", [D, NR * D], "bfloat16"),
    "zero": ("sbuf", [D, KB * D], "float32"),
    "qd": ("dram", [D, D], "bfloat16"),
    "qr": ("dram", [D, D], "bfloat16"),
    "yd": ("dram", [D, D], "bfloat16"),
}
for _b in range(NBANK):
    SCRATCH["ps%d" % _b] = ("psum", [D, 512], "float32")
    SCRATCH["po%d" % _b] = ("psum", [D, 512], "float32")

SEMAPHORES = ["kld", "vld", "kar", "var", "qld", "qrel", "zr", "sent", "yarr", "st"]
SEMAPHORES += ["qa%d" % r for r in range(NR)]
SEMAPHORES += ["%s%d" % (s, i) for s in ("sS", "sR", "sO", "sY") for i in range(NR)]


def _pick(mask, n, avoid=0):
    bits = [b for b in range(mask.bit_length()) if (mask >> b) & 1]
    bits.sort(key=lambda b: ((avoid >> b) & 1, b))
    m = 0
    for b in bits[:n]:
        m |= 1 << b
    return m


def _plan(T, topo):
    cores = list(T.cores)
    mem = cores[T.tables["MEM"][0]]
    home = topo.chip(mem)
    near = [c for c in cores if c != mem and topo.chip(c) == home]
    far = [c for c in cores if topo.chip(c) != home]
    cand = [c for c in range(NSIM) if topo.chip(c) == home and c != mem
            and all(topo.may_write(c, f) for f in far)]
    cand.sort(key=lambda c: (topo.die(c) == topo.die(mem), c))
    helpers = cand[:NHELP]
    direct = [c for c in far if topo.may_write(c, mem)]
    indirect = [c for c in far if not topo.may_write(c, mem)]
    relay = {}
    for c in indirect:
        opts = [d for d in direct if topo.chip(d) == topo.chip(c)]
        relay[c] = min(opts, key=lambda d: (sum(1 for x in opts if topo.die(x) == topo.die(d)), d))
    pos = {}
    for c in direct:
        pos[c] = sum(1 for x in direct if topo.chip(x) == topo.chip(c) and x < c)
    direct = sorted(direct, key=lambda c: (c in relay.values(), pos[c], c))
    first = {mem: near + direct[:NMEM_FAR]}
    rest = direct[NMEM_FAR:]
    for j, h in enumerate(helpers):
        first[h] = rest[j::len(helpers)]
    late = {s: [] for s in first}
    turn = [mem] + helpers[::-1]
    for k, c in enumerate(indirect):
        late[turn[k % len(turn)]].append(c)
    late[mem].append(mem)
    serve = {s: [first[s], late[s]] for s in first}
    server = {}
    for s in serve:
        for w in serve[s]:
            for c in w:
                server[c] = s
    return {"mem": mem, "helpers": helpers, "far": far, "relay": relay, "serve": serve, "server": server}


def rank_program(g, core, T, topo):
    P = _plan(T, topo)
    rank = T.rank_of(core)
    if rank is None and core not in P["serve"]:
        return
    sem = T.sem
    mem = P["mem"]
    sent = [0]
    stored = [0]
    client = rank is not None and P["server"][core] != core

    def write(dst, out_ap, in_ap, remote_sem, n, avoid=0):
        rid, pid, _se = topo.addr(dst)
        g.remote_dma(out_ap=out_ap, in_ap=in_ap, remote_sem=remote_sem, local_sem=sem.sent, pid=pid, routing_id=rid,
                     dma_engine_mask=_pick(topo.mask(core, dst), n, avoid))
        sent[0] += n

    def qslot(r):
        return T.qin[:, r * D:(r + 1) * D]

    if client:
        g.sync.dma_start(T.qd[:], T.q[:]).then_inc(sem.qld, 16)
        g.wait_ge(sem.qld, 16)
        if core in P["relay"]:
            write(P["relay"][core], T.qr[:], T.qd[:], sem.qrel, NE_RELAY)
        else:
            write(P["server"][core], qslot(rank), T.qd[:], sem["qa%d" % rank], NE_Q)
        for c in P["relay"]:
            if P["relay"][c] == core:
                g.wait_ge(sem.qrel, NE_RELAY)
                write(P["server"][c], qslot(T.rank_of(c)), T.qr[:], sem["qa%d" % T.rank_of(c)], NE_Q)

    if core in P["serve"]:
        waves = [w for w in P["serve"][core] if w]
        order = [c for w in waves for c in w]
        if core == mem:
            g.sync.dma_start(T.kk[:], T.k[:]).then_inc(sem.kld, 16)
            g.sync.dma_start(T.vv[:], T.v[:]).then_inc(sem.vld, 16)
            k_sem, v_sem, kv_cnt = sem.kld, sem.vld, 16
        else:
            k_sem, v_sem, kv_cnt = sem.kar, sem.var, NE_KV
        if core in order:
            g.sync.dma_start(qslot(rank), T.q[:]).then_inc(sem.qld, 16)
        g.vector.memset(T.zero[:], 0.0).then_inc(sem.zr, 1)
        g.vector.wait_ge(sem.zr, 1)
        g.tensor.wait_ge(k_sem, kv_cnt)

        def scores(i):
            c = order[i]
            r = T.rank_of(c)
            if c == core:
                g.tensor.wait_ge(sem.qld, 16)
            else:
                g.tensor.wait_ge(sem["qa%d" % r], NE_Q)
            ps = T["ps%d" % (i % NBANK)]
            for b in range(KB):
                g.tensor.matmul(ps[:, b * D:(b + 1) * D], T.kk[:, b * D:(b + 1) * D], qslot(r),
                                start=True, stop=True).then_inc(sem["sS%d" % i], 1)
            g.vector.wait_ge(sem["sS%d" % i], KB)
            g.vector.tensor_tensor(T.sact[:, i * KB * D:(i + 1) * KB * D], ps[:], T.zero[:],
                                   AluOpType.max).then_inc(sem["sR%d" % i], 1)

        def outs(i):
            if i == 0:
                g.tensor.wait_ge(v_sem, kv_cnt)
            g.tensor.wait_ge(sem["sR%d" % i], 1)
            if i >= NBANK:
                g.tensor.wait_ge(sem["sY%d" % (i - NBANK)], 1)
            po = T["po%d" % (i % NBANK)]
            for b in range(KB):
                g.tensor.matmul(po[:, 0:D], T.vv[:, b * D:(b + 1) * D],
                                T.sact[:, (i * KB + b) * D:(i * KB + b + 1) * D],
                                start=(b == 0), stop=(b == KB - 1)).then_inc(sem["sO%d" % i], 1)
            g.vector.wait_ge(sem["sO%d" % i], KB)
            g.vector.tensor_copy(T.yo[:, i * D:(i + 1) * D], po[:, 0:D]).then_inc(sem["sY%d" % i], 1)

        base = 0
        for w in waves:
            for j in range(len(w) + 1):
                if j < len(w):
                    scores(base + j)
                if j >= 1:
                    outs(base + j - 1)
            base += len(w)
        if core == mem and P["helpers"]:
            g.wait_ge(sem.kld, 16)
            for h in P["helpers"]:
                write(h, T.kk[:], T.kk[:], sem.kar, NE_KV)
            g.wait_ge(sem.vld, 16)
            for h in P["helpers"]:
                write(h, T.vv[:], T.vv[:], sem.var, NE_KV)
        far_mask = topo.mask(core, P["far"][0])
        for i, c in enumerate(order):
            if c == core:
                g.sync.wait_ge(sem["sY%d" % i], 1)
                g.sync.dma_start(T.y[:], T.yo[:, i * D:(i + 1) * D]).then_inc(sem.st, 16)
                stored[0] += 16
            else:
                g.wait_ge(sem["sY%d" % i], 1)
                write(c, T.yd[:], T.yo[:, i * D:(i + 1) * D], sem.yarr, NE_Y,
                      avoid=far_mask if topo.chip(c) == topo.chip(core) else 0)

    if client:
        g.sync.wait_ge(sem.yarr, NE_Y)
        g.sync.dma_start(T.y[:], T.yd[:]).then_inc(sem.st, 16)
        stored[0] += 16

    if sent[0]:
        g.wait_ge(sem.sent, sent[0])
    if stored[0]:
        g.wait_ge(sem.st, stored[0])
